import numpy as np
import ml_dtypes


def mxq(x, axis, fmt="e4m3"):
    dtype, down = {"e4m3": (ml_dtypes.float8_e4m3fn, 7), "e5m2": (ml_dtypes.float8_e5m2, 14)}[fmt]
    v = np.moveaxis(np.asarray(x, np.float32).astype(ml_dtypes.bfloat16).astype(np.float64), axis, -1)
    blocks = v.reshape(v.shape[:-1] + (-1, 32))
    amax = np.abs(blocks).max(-1, keepdims=True)
    byte = np.maximum(np.where(amax > 0, np.frexp(amax)[1] - 1 + 127, 0) - down, 1)
    scale = np.exp2(byte - 127.0)
    codes = (blocks / scale).astype(np.float32).astype(dtype).astype(np.float64)
    return np.moveaxis((codes * scale).reshape(v.shape), -1, axis)


WIDE = False


def mx_kscale(k):
    if not WIDE:
        return np.ones(k)
    levels = np.array([10, -10, 5, -5, 0])
    if k % 512:
        return np.exp2(np.random.permutation(np.resize(levels, k // 32))).repeat(32)
    a = np.empty((k // 512, 16))
    for p in range(k // 512):
        a[p, :8] = np.random.permutation(np.resize(levels, 8))
        for g in range(8):
            far = levels[np.abs(levels - a[p, g]) >= 10]
            a[p, g + 8] = far[np.random.randint(len(far))]
    return np.exp2(a.ravel()).repeat(32)


def f64(x):
    return np.asarray(x).astype(np.float64)


def striped(idx):
    return np.tile(idx.reshape(-1, 16).T, (8, 1)).astype(np.uint16)


def unstriped(offs):
    return offs[:16].T.reshape(-1).astype(np.int64)


K, T, E, C, N = 1024, 768, 4, 128, 384


def by_expert(wq, xq):
    return np.concatenate([wq[e].T @ xq[:, e * C:(e + 1) * C] for e in range(E)], axis=1)


def setup_inputs():
    n = np.random.standard_normal
    s = mx_kscale(K)[:, None]
    return {
        "xT": (n((K, T)) * s).astype(np.float32),
        "w": (n((E + 1, K, N)) / np.sqrt(K) / s[None]).astype(np.float32),
        "b": (0.3 * n((N, E + 1))).astype(np.float32),
        "gate": np.tile(np.random.uniform(0.2, 1.0, E * C), (N, 1)).astype(np.float32),
        "offs": striped(np.random.permutation(T)[:E * C]),
    }


def reference(xT, w, b, gate, offs):
    idx = unstriped(offs)
    wq = mxq(f64(w), 1, "e4m3")
    xs = mxq(f64(xT), 0, "e4m3")
    ys = (wq[E].T @ xs) + f64(b)[:, E:]
    xq = mxq(f64(xT)[:, idx], 0, "e4m3")
    y = by_expert(wq, xq)
    y = y + np.repeat(f64(b)[:, :E], C, axis=1)
    out = ys
    out[:, idx] += f64(gate) * y
    return out

@@ -1,0 +1,207 @@
+from contextlib import ExitStack
+
+import concourse.mybir as mybir
+
+K, T, E, C, N = 1024, 768, 4, 128, 384
+S = E * C
+
+F32 = mybir.dt.float32
+BF16 = mybir.dt.bfloat16
+U32 = mybir.dt.uint32
+U16 = mybir.dt.uint16
+U8 = mybir.dt.uint8
+FP8X4 = mybir.dt.float8_e4m3fn_x4
+ADD = mybir.AluOpType.add
+MULT = mybir.AluOpType.mult
+IDENT = mybir.ActivationFunctionType.Identity
+
+P = 128
+PACK = 4
+K_PASS = P * PACK
+PASSES = K // K_PASS
+NT = N // P
+BANK = 512
+
+FLOPS = 2 * K * N * (S + T)
+
+
+def tile_moe_shr_lin_bias_kernel(tc, xT, w, b, gate, offs, out):
+    nc = tc.nc
+    with ExitStack() as ctx:
+        keep = ctx.enter_context(tc.tile_pool(name="keep", bufs=1))
+        psum = ctx.enter_context(tc.psum_pool(name="psum", bufs=1))
+        psum_r = ctx.enter_context(tc.psum_pool(name="psum_r", bufs=2))
+
+        offsets = keep.tile([P, S // 16], U16, name="offsets")
+        x_raw = [[keep.tile([P, 2, T], F32, name=f"x_raw{g}{u}") for u in range(2)] for g in range(PASSES)]
+        w_raw = [[keep.tile([P, PACK, N], F32, name=f"w_raw{e}{g}") for g in range(PASSES)] for e in range(E + 1)]
+        bias = keep.tile([P, NT, E + 1], F32, name="bias")
+        gates = keep.tile([P, NT, S], F32, name="gates")
+
+        def load_x(g, u):
+            rows = xT[g * K_PASS:(g + 1) * K_PASS, :].rearrange("(p j) t -> p j t", j=PACK)
+            nc.sync.dma_start(out=x_raw[g][u][:], in_=rows[:, 2 * u:2 * u + 2, :])
+
+        def load_w(e, g):
+            rows = w[e, g * K_PASS:(g + 1) * K_PASS, :].rearrange("(p j) n -> p j n", j=PACK)
+            nc.sync.dma_start(out=w_raw[e][g][:], in_=rows)
+
+        load_x(0, 0)
+        nc.sync.dma_start(offsets[:], offs)
+        load_x(0, 1)
+        load_x(1, 0)
+        load_x(1, 1)
+        load_w(0, 0)
+        load_w(0, 1)
+        nc.sync.dma_start(out=bias[:], in_=b.rearrange("(m p) e -> p m e", p=P))
+        load_w(1, 0)
+        nc.sync.dma_start(out=gates[:, 0, :], in_=gate[0:P, :])
+        load_w(1, 1)
+        nc.sync.dma_start(out=gates[:, 1:, :], in_=gate[P:, :].rearrange("(m p) s -> p m s", p=P))
+        for e in range(2, E + 1):
+            for g in range(PASSES):
+                load_w(e, g)
+
+        warm = keep.tile([P, 8], F32, name="warm")
+        warm_out = keep.tile([P, 8], F32, name="warm_out")
+        nc.vector.memset(warm[:], 0.0)
+        nc.scalar.activation(warm_out[:], warm[:], IDENT, bias=warm[:, 0:1])
+        routed = [keep.tile([P, T], F32, name=f"routed{m}") for m in range(NT)]
+        for m in range(NT):
+            nc.vector.memset(routed[m][:], 0.0)
+
+        x_pairs = [keep.tile([P, 2, T, 2], BF16, name=f"x_pairs{g}") for g in range(PASSES)]
+        s_pairs = [keep.tile([P, 2, S, 2], BF16, name=f"s_pairs{g}") for g in range(PASSES)]
+        w_quad = [keep.tile([P, PASSES, N, PACK], BF16, name=f"w_quad{e}", align_bytes=64) for e in range(E + 1)]
+        x_quad0 = keep.tile([P, T, 2, 2], BF16, name="x_quad0", align_bytes=64)
+        x_quad = [x_quad0[:], w_quad[0][:].rearrange("p g n j -> p (g n j)").rearrange("p (c u e) -> p c u e", u=2, e=2)]
+        s_quad = [keep.tile([P, S, 2, 2], BF16, name=f"s_quad{g}", align_bytes=64) for g in range(PASSES)]
+        x_codes = keep.tile([P, PASSES, T], U32, name="x_codes", align_bytes=64)
+        x_scales = keep.tile([P, PASSES, T], U8, name="x_scales", align_bytes=64)
+        s_codes = keep.tile([P, PASSES, S], U32, name="s_codes", align_bytes=64)
+        s_scales = keep.tile([P, PASSES, S], U8, name="s_scales", align_bytes=64)
+
+        def cast_x(g, u, on_vector):
+            src = x_raw[g][u][:].rearrange("p e t -> p t e")
+            if on_vector:
+                nc.vector.tensor_copy(out=x_pairs[g][:, u, :on_vector, :], in_=src[:, :on_vector, :])
+            nc.scalar.copy(out=x_pairs[g][:, u, on_vector:, :], in_=src[:, on_vector:, :])
+
+        def gather(g, u):
+            window = x_pairs[g][:, u, :, :].rearrange("p t e -> p (t e)").bitcast(U32)
+            dst = s_pairs[g][:, u, :, :].rearrange("p s e -> p (s e)").bitcast(U32)
+            nc.vector.tensor_copy(dst, window.indirect(offsets[:]))
+
+        def quantize(codes, scales, quad, lo, hi):
+            nc.vector.quantize_mx(
+                out=codes[:, lo:hi].bitcast(FP8X4), scales=scales[:, lo:hi], in_=quad[:, PACK * lo:PACK * hi]
+            )
+
+        def join_pairs(quad, pairs):
+            nc.vector.tensor_copy(out=quad, in_=pairs[:].rearrange("p u c e -> p c u e"))
+
+        def flat(quad):
+            return quad.rearrange("p c u e -> p (c u e)")
+
+        def quantize_tokens(g):
+            quantize(x_codes[:, g, :], x_scales[:, g, :], flat(x_quad[g]), 0, 512)
+            quantize(x_codes[:, g, :], x_scales[:, g, :], flat(x_quad[g]), 512, T)
+
+        for g in range(PASSES):
+            for u in range(2):
+                cast_x(g, u, 512 if g == 0 else 0)
+                gather(g, u)
+            join_pairs(s_quad[g][:], s_pairs[g])
+            if g == 0:
+                join_pairs(x_quad[g], x_pairs[g])
+            quantize(s_codes[:, g, :], s_scales[:, g, :], flat(s_quad[g][:]), 0, S)
+        quantize_tokens(0)
+
+        w_codes = [keep.tile([P, PASSES * N], U32, name=f"w_codes{e}", align_bytes=64) for e in range(E + 1)]
+        w_scales = [keep.tile([P, PASSES * N], U8, name=f"w_scales{e}", align_bytes=64) for e in range(E + 1)]
+
+        def cast_w(e, g, lo=0, hi=N):
+            nc.scalar.copy(
+                out=w_quad[e][:, g, lo:hi, :].rearrange("p (c i) j -> p c j i", i=4),
+                in_=w_raw[e][g][:, :, lo:hi].rearrange("p j (c i) -> p c j i", i=4),
+            )
+
+        def quantize_w(e):
+            quad = w_quad[e][:].rearrange("p g n j -> p (g n j)")
+            quantize(w_codes[e], w_scales[e], quad, 0, 256)
+            quantize(w_codes[e], w_scales[e], quad, 256, PASSES * N)
+
+        def product(acc, e, m, codes, scales, lo, hi):
+            for g in range(PASSES):
+                cols = slice(g * N + m * P, g * N + (m + 1) * P)
+                nc.tensor.matmul_mx(
+                    out=acc,
+                    lhsT=w_codes[e][:, cols].bitcast(FP8X4),
+                    lhsT_scale=w_scales[e][:, cols],
+                    rhs=codes[:, g, lo:hi].bitcast(FP8X4),
+                    rhs_scale=scales[:, g, lo:hi],
+                    start=(g == 0),
+                    stop=(g == PASSES - 1),
+                )
+
+        def multiply_slots(e):
+            acc = psum_r.tile([P, NT, C], F32, name="acc")
+            for m in range(NT):
+                product(acc[:, m, :], e, m, s_codes, s_scales, e * C, (e + 1) * C)
+            return acc
+
+        def y_of(e, m):
+            return w_raw[e + 1][0 if m == 0 or e == E - 1 else 1][:, m, :C]
+
+        def add_bias(e, acc, m):
+            nc.scalar.activation(y_of(e, m), acc[:, m, :], IDENT, bias=bias[:, m, e:e + 1])
+
+        def scatter(e, m):
+            nc.vector.tensor_tensor(
+                routed[m][:].indirect(offsets[:, e * C // 16:(e + 1) * C // 16]),
+                y_of(e, m),
+                gates[:, m, e * C:(e + 1) * C],
+                MULT,
+            )
+
+        cast_w(0, 0)
+        cast_w(0, 1)
+        quantize_w(0)
+        acc = multiply_slots(0)
+        join_pairs(x_quad[1], x_pairs[1])
+        quantize_tokens(1)
+        for e in range(E - 1):
+            cast_w(e + 1, 0)
+            add_bias(e, acc, 0)
+            scatter(e, 0)
+            cast_w(e + 1, 1)
+            quantize_w(e + 1)
+            for m in (1, 2):
+                add_bias(e, acc, m)
+                scatter(e, m)
+            acc = multiply_slots(e + 1)
+
+        shared_quad = w_quad[E][:].rearrange("p g n j -> p (g n j)")
+        cast_w(E, 0)
+        for m in range(NT):
+            add_bias(E - 1, acc, m)
+        quantize(w_codes[E], w_scales[E], shared_quad, 0, 256)
+        quantize(w_codes[E], w_scales[E], shared_quad, 256, N)
+        for m in range(NT):
+            scatter(E - 1, m)
+        for m in range(NT):
+            cast_w(E, 1, m * P, (m + 1) * P)
+            quantize(w_codes[E], w_scales[E], shared_quad, N + m * P, N + (m + 1) * P)
+
+        result = keep.tile([P, NT, T], F32, name="result")
+        for m in range(NT):
+            for lo, hi in ((0, BANK), (BANK, T)):
+                shared = psum.tile([P, hi - lo], F32, name=f"shared{m}_{lo}")
+                product(shared[:], E, m, x_codes, x_scales, lo, hi)
+                nc.vector.scalar_tensor_tensor(
+                    result[:, m, lo:hi], shared[:], bias[:, m, E:E + 1], routed[m][:, lo:hi], ADD, ADD
+                )
+                if m == NT - 1:
+                    nc.sync.dma_start(out=out[m * P:(m + 1) * P, lo:hi], in_=result[:, m, lo:hi])
+            if m < NT - 1:
+                nc.sync.dma_start(out=out[m * P:(m + 1) * P, :], in_=result[:, m, :])

@@ -30,30 +30,30 @@ def tile_moe_shr_lin_bias_kernel(tc, xT, w, b, gate, offs, out):
     with ExitStack() as ctx:
         keep = ctx.enter_context(tc.tile_pool(name="keep", bufs=1))
         psum = ctx.enter_context(tc.psum_pool(name="psum", bufs=1))
-        psum_r = ctx.enter_context(tc.psum_pool(name="psum_r", bufs=2))
 
         offsets = keep.tile([P, S // 16], U16, name="offsets")
         x_raw = [[keep.tile([P, 2, T], F32, name=f"x_raw{g}{u}") for u in range(2)] for g in range(PASSES)]
         w_raw = [[keep.tile([P, PACK, N], F32, name=f"w_raw{e}{g}") for g in range(PASSES)] for e in range(E + 1)]
-        bias = keep.tile([P, NT, E + 1], F32, name="bias")
+        bias = keep.tile([P, NT, 8], F32, name="bias")
         gates = keep.tile([P, NT, S], F32, name="gates")
 
-        def load_x(g, u):
+        def load_x(g, u, lo=0, hi=T):
             rows = xT[g * K_PASS:(g + 1) * K_PASS, :].rearrange("(p j) t -> p j t", j=PACK)
-            nc.sync.dma_start(out=x_raw[g][u][:], in_=rows[:, 2 * u:2 * u + 2, :])
+            nc.sync.dma_start(out=x_raw[g][u][:, :, lo:hi], in_=rows[:, 2 * u:2 * u + 2, lo:hi])
 
         def load_w(e, g):
             rows = w[e, g * K_PASS:(g + 1) * K_PASS, :].rearrange("(p j) n -> p j n", j=PACK)
             nc.sync.dma_start(out=w_raw[e][g][:], in_=rows)
 
-        load_x(0, 0)
+        load_x(0, 0, 0, T // 2)
+        load_x(0, 0, T // 2, T)
         nc.sync.dma_start(offsets[:], offs)
         load_x(0, 1)
         load_x(1, 0)
         load_x(1, 1)
         load_w(0, 0)
         load_w(0, 1)
-        nc.sync.dma_start(out=bias[:], in_=b.rearrange("(m p) e -> p m e", p=P))
+        nc.sync.dma_start(out=bias[:, :, :E + 1], in_=b.rearrange("(m p) e -> p m e", p=P))
         load_w(1, 0)
         nc.sync.dma_start(out=gates[:, 0, :], in_=gate[0:P, :])
         load_w(1, 1)
@@ -72,20 +72,18 @@ def tile_moe_shr_lin_bias_kernel(tc, xT, w, b, gate, offs, out):
 
         x_pairs = [keep.tile([P, 2, T, 2], BF16, name=f"x_pairs{g}") for g in range(PASSES)]
         s_pairs = [keep.tile([P, 2, S, 2], BF16, name=f"s_pairs{g}") for g in range(PASSES)]
-        w_quad = [keep.tile([P, PASSES, N, PACK], BF16, name=f"w_quad{e}", align_bytes=64) for e in range(E + 1)]
+        w_quad = [keep.tile([P, NT * PASSES, P, PACK], BF16, name=f"w_quad{e}", align_bytes=64) for e in range(E + 1)]
         x_quad0 = keep.tile([P, T, 2, 2], BF16, name="x_quad0", align_bytes=64)
-        x_quad = [x_quad0[:], w_quad[0][:].rearrange("p g n j -> p (g n j)").rearrange("p (c u e) -> p c u e", u=2, e=2)]
+        w0_bytes = w_quad[0][:].rearrange("p q n j -> p (q n j)")
+        x_quad = [x_quad0[:], w0_bytes.rearrange("p (c u e) -> p c u e", u=2, e=2)]
         s_quad = [keep.tile([P, S, 2, 2], BF16, name=f"s_quad{g}", align_bytes=64) for g in range(PASSES)]
         x_codes = keep.tile([P, PASSES, T], U32, name="x_codes", align_bytes=64)
         x_scales = keep.tile([P, PASSES, T], U8, name="x_scales", align_bytes=64)
         s_codes = keep.tile([P, PASSES, S], U32, name="s_codes", align_bytes=64)
         s_scales = keep.tile([P, PASSES, S], U8, name="s_scales", align_bytes=64)
 
-        def cast_x(g, u, on_vector):
-            src = x_raw[g][u][:].rearrange("p e t -> p t e")
-            if on_vector:
-                nc.vector.tensor_copy(out=x_pairs[g][:, u, :on_vector, :], in_=src[:, :on_vector, :])
-            nc.scalar.copy(out=x_pairs[g][:, u, on_vector:, :], in_=src[:, on_vector:, :])
+        def cast_x(copy, g, u, lo, hi):
+            copy(out=x_pairs[g][:, u, lo:hi, :], in_=x_raw[g][u][:, :, lo:hi].rearrange("p e t -> p t e"))
 
         def gather(g, u):
             window = x_pairs[g][:, u, :, :].rearrange("p t e -> p (t e)").bitcast(U32)
@@ -97,43 +95,61 @@ def tile_moe_shr_lin_bias_kernel(tc, xT, w, b, gate, offs, out):
                 out=codes[:, lo:hi].bitcast(FP8X4), scales=scales[:, lo:hi], in_=quad[:, PACK * lo:PACK * hi]
             )
 
-        def join_pairs(quad, pairs):
-            nc.vector.tensor_copy(out=quad, in_=pairs[:].rearrange("p u c e -> p c u e"))
+        def join_pairs(copy, quad, pairs, lo, hi):
+            copy(out=quad[:, lo:hi, :, :], in_=pairs[:, :, lo:hi, :].rearrange("p u c e -> p c u e"))
 
         def flat(quad):
             return quad.rearrange("p c u e -> p (c u e)")
 
-        def quantize_tokens(g):
-            quantize(x_codes[:, g, :], x_scales[:, g, :], flat(x_quad[g]), 0, 512)
-            quantize(x_codes[:, g, :], x_scales[:, g, :], flat(x_quad[g]), 512, T)
+        def quantize_tokens(g, lo, hi):
+            quantize(x_codes[:, g, :], x_scales[:, g, :], flat(x_quad[g]), lo, hi)
 
-        for g in range(PASSES):
-            for u in range(2):
-                cast_x(g, u, 512 if g == 0 else 0)
-                gather(g, u)
-            join_pairs(s_quad[g][:], s_pairs[g])
-            if g == 0:
-                join_pairs(x_quad[g], x_pairs[g])
+        def quantize_slots(g):
             quantize(s_codes[:, g, :], s_scales[:, g, :], flat(s_quad[g][:]), 0, S)
-        quantize_tokens(0)
+
+        on_vector, on_scalar = nc.vector.tensor_copy, nc.scalar.copy
+        cast_x(on_vector, 0, 0, 0, 384)
+        cast_x(on_vector, 0, 0, 384, 640)
+        cast_x(on_scalar, 0, 0, 640, T)
+        gather(0, 0)
+        cast_x(on_vector, 0, 1, 0, 512)
+        cast_x(on_scalar, 0, 1, 512, T)
+        gather(0, 1)
+        join_pairs(on_vector, x_quad[0], x_pairs[0], 0, 512)
+        join_pairs(on_scalar, x_quad[0], x_pairs[0], 512, T)
+        join_pairs(on_vector, s_quad[0], s_pairs[0], 0, S)
+        for u in range(2):
+            cast_x(on_scalar, 1, u, 0, T)
+            gather(1, u)
+        quantize_tokens(0, 0, 512)
+        quantize_slots(0)
+        join_pairs(on_vector, s_quad[1], s_pairs[1], 0, S)
+        quantize_tokens(0, 512, T)
+        quantize_slots(1)
 
         w_codes = [keep.tile([P, PASSES * N], U32, name=f"w_codes{e}", align_bytes=64) for e in range(E + 1)]
         w_scales = [keep.tile([P, PASSES * N], U8, name=f"w_scales{e}", align_bytes=64) for e in range(E + 1)]
 
-        def cast_w(e, g, lo=0, hi=N):
-            nc.scalar.copy(
-                out=w_quad[e][:, g, lo:hi, :].rearrange("p (c i) j -> p c j i", i=4),
-                in_=w_raw[e][g][:, :, lo:hi].rearrange("p j (c i) -> p c j i", i=4),
+        def block(e, m, g):
+            return g * NT + m if e == E else m * PASSES + g
+
+        def cast_w(e, g, copy=on_scalar, lo=0, hi=NT):
+            if e == E:
+                dst = w_quad[e][:, g * NT:(g + 1) * NT, :, :]
+            else:
+                dst = w_quad[e][:, g::PASSES, :, :]
+            copy(
+                out=dst[:, lo:hi, :, :].rearrange("p m (c i) j -> p m c j i", i=4),
+                in_=w_raw[e][g][:, :, lo * P:hi * P].rearrange("p j (m c i) -> p m c j i", c=P // 4, i=4),
             )
 
-        def quantize_w(e):
-            quad = w_quad[e][:].rearrange("p g n j -> p (g n j)")
-            quantize(w_codes[e], w_scales[e], quad, 0, 256)
-            quantize(w_codes[e], w_scales[e], quad, 256, PASSES * N)
+        def quantize_w(e, lo, hi):
+            quad = w_quad[e][:].rearrange("p q n j -> p (q n j)")
+            quantize(w_codes[e], w_scales[e], quad, lo * P, hi * P)
 
         def product(acc, e, m, codes, scales, lo, hi):
             for g in range(PASSES):
-                cols = slice(g * N + m * P, g * N + (m + 1) * P)
+                cols = slice(block(e, m, g) * P, (block(e, m, g) + 1) * P)
                 nc.tensor.matmul_mx(
                     out=acc,
                     lhsT=w_codes[e][:, cols].bitcast(FP8X4),
@@ -145,16 +161,18 @@ def tile_moe_shr_lin_bias_kernel(tc, xT, w, b, gate, offs, out):
                 )
 
         def multiply_slots(e):
-            acc = psum_r.tile([P, NT, C], F32, name="acc")
+            first = psum.tile([P, C], F32, name="first")
+            rest = psum.tile([P, NT - 1, C], F32, name="rest")
+            accs = [first[:]] + [rest[:, m, :] for m in range(NT - 1)]
             for m in range(NT):
-                product(acc[:, m, :], e, m, s_codes, s_scales, e * C, (e + 1) * C)
-            return acc
+                product(accs[m], e, m, s_codes, s_scales, e * C, (e + 1) * C)
+            return accs
 
         def y_of(e, m):
-            return w_raw[e + 1][0 if m == 0 or e == E - 1 else 1][:, m, :C]
+            return w_raw[e + 1][min(m, 1)][:, PACK - 1, m * P:(m + 1) * P]
 
-        def add_bias(e, acc, m):
-            nc.scalar.activation(y_of(e, m), acc[:, m, :], IDENT, bias=bias[:, m, e:e + 1])
+        def add_bias(e, accs, m):
+            nc.scalar.activation(y_of(e, m), accs[m], IDENT, bias=bias[:, m, e:e + 1])
 
         def scatter(e, m):
             nc.vector.tensor_tensor(
@@ -166,42 +184,49 @@ def tile_moe_shr_lin_bias_kernel(tc, xT, w, b, gate, offs, out):
 
         cast_w(0, 0)
         cast_w(0, 1)
-        quantize_w(0)
-        acc = multiply_slots(0)
-        join_pairs(x_quad[1], x_pairs[1])
-        quantize_tokens(1)
-        for e in range(E - 1):
+        quantize_w(0, 0, 2)
+        quantize_w(0, 2, 6)
+        accs = multiply_slots(0)
+        join_pairs(on_vector, x_quad[1], x_pairs[1], 0, T)
+        quantize_tokens(1, 0, 512)
+        quantize_tokens(1, 512, T)
+        for e in range(E):
             cast_w(e + 1, 0)
-            add_bias(e, acc, 0)
+            add_bias(e, accs, 0)
+            if e + 1 == E:
+                quantize_w(E, 0, 2)
+                quantize_w(E, 2, 3)
             scatter(e, 0)
-            cast_w(e + 1, 1)
-            quantize_w(e + 1)
-            for m in (1, 2):
-                add_bias(e, acc, m)
+            if e + 1 == E:
+                cast_w(E, 1, on_scalar, 2, 3)
+                cast_w(E, 1, on_vector, 0, 2)
+                quantize_w(E, 5, 6)
+                quantize_w(E, 3, 5)
+            else:
+                cast_w(e + 1, 1)
+                quantize_w(e + 1, 0, 2)
+                quantize_w(e + 1, 2, 6)
+            for m in range(1, NT):
+                add_bias(e, accs, m)
                 scatter(e, m)
-            acc = multiply_slots(e + 1)
-
-        shared_quad = w_quad[E][:].rearrange("p g n j -> p (g n j)")
-        cast_w(E, 0)
-        for m in range(NT):
-            add_bias(E - 1, acc, m)
-        quantize(w_codes[E], w_scales[E], shared_quad, 0, 256)
-        quantize(w_codes[E], w_scales[E], shared_quad, 256, N)
-        for m in range(NT):
-            scatter(E - 1, m)
-        for m in range(NT):
-            cast_w(E, 1, m * P, (m + 1) * P)
-            quantize(w_codes[E], w_scales[E], shared_quad, N + m * P, N + (m + 1) * P)
+            if e + 1 < E:
+                accs = multiply_slots(e + 1)
 
         result = keep.tile([P, NT, T], F32, name="result")
-        for m in range(NT):
-            for lo, hi in ((0, BANK), (BANK, T)):
-                shared = psum.tile([P, hi - lo], F32, name=f"shared{m}_{lo}")
-                product(shared[:], E, m, x_codes, x_scales, lo, hi)
+        ys = keep.tile([P, BANK], F32, name="ys")
+        last = NT - 1
+        pieces = [(last, 0, BANK)] + [(m, lo, hi) for m in range(last) for lo, hi in ((0, BANK), (BANK, T))]
+        for m, lo, hi in pieces + [(last, BANK, T)]:
+            shared = psum.tile([P, hi - lo], F32, name=f"shared{m}_{lo}")
+            product(shared[:], E, m, x_codes, x_scales, lo, hi)
+            if (m, lo) == (last, 0):
+                nc.scalar.activation(ys[:], shared[:], IDENT, bias=bias[:, m, E:E + 1])
+                nc.gpsimd.tensor_tensor(result[:, m, lo:hi], ys[:], routed[m][:, lo:hi], ADD)
+            else:
                 nc.vector.scalar_tensor_tensor(
                     result[:, m, lo:hi], shared[:], bias[:, m, E:E + 1], routed[m][:, lo:hi], ADD, ADD
                 )
-                if m == NT - 1:
-                    nc.sync.dma_start(out=out[m * P:(m + 1) * P, lo:hi], in_=result[:, m, lo:hi])
-            if m < NT - 1:
+            if m < last and hi == T:
                 nc.sync.dma_start(out=out[m * P:(m + 1) * P, :], in_=result[:, m, :])
+        for lo, hi in ((0, BANK), (BANK, T)):
+            nc.sync.dma_start(out=out[last * P:, lo:hi], in_=result[:, last, lo:hi])

@@ -53,14 +53,21 @@ def tile_moe_shr_lin_bias_kernel(tc, xT, w, b, gate, offs, out):
         load_x(1, 1)
         load_w(0, 0)
         load_w(0, 1)
-        nc.sync.dma_start(out=bias[:, :, :E + 1], in_=b.rearrange("(m p) e -> p m e", p=P))
+        gate_rows = gate.rearrange("(m p) s -> p m s", p=P)
+        half = S // 2
         load_w(1, 0)
-        nc.sync.dma_start(out=gates[:, 0, :], in_=gate[0:P, :])
+        nc.sync.dma_start(out=bias[:, :, :E + 1], in_=b.rearrange("(m p) e -> p m e", p=P))
+        nc.sync.dma_start(out=gates[:, :1, :half], in_=gate_rows[:, :1, :half])
         load_w(1, 1)
-        nc.sync.dma_start(out=gates[:, 1:, :], in_=gate[P:, :].rearrange("(m p) s -> p m s", p=P))
-        for e in range(2, E + 1):
-            for g in range(PASSES):
-                load_w(e, g)
+        nc.sync.dma_start(out=gates[:, 1:, :half], in_=gate_rows[:, 1:, :half])
+        load_w(2, 0)
+        load_w(2, 1)
+        nc.sync.dma_start(out=gates[:, :1, half:], in_=gate_rows[:, :1, half:])
+        load_w(3, 0)
+        load_w(3, 1)
+        nc.sync.dma_start(out=gates[:, 1:, half:], in_=gate_rows[:, 1:, half:])
+        load_w(4, 0)
+        load_w(4, 1)
 
         warm = keep.tile([P, 8], F32, name="warm")
         warm_out = keep.tile([P, 8], F32, name="warm_out")
@@ -187,7 +194,8 @@ def tile_moe_shr_lin_bias_kernel(tc, xT, w, b, gate, offs, out):
         quantize_w(0, 0, 2)
         quantize_w(0, 2, 6)
         accs = multiply_slots(0)
-        join_pairs(on_vector, x_quad[1], x_pairs[1], 0, T)
+        join_pairs(on_vector, x_quad[1], x_pairs[1], 0, 512)
+        join_pairs(on_vector, x_quad[1], x_pairs[1], 512, T)
         quantize_tokens(1, 0, 512)
         quantize_tokens(1, 512, T)
         for e in range(E):
@@ -195,13 +203,10 @@ def tile_moe_shr_lin_bias_kernel(tc, xT, w, b, gate, offs, out):
             add_bias(e, accs, 0)
             if e + 1 == E:
                 quantize_w(E, 0, 2)
-                quantize_w(E, 2, 3)
             scatter(e, 0)
             if e + 1 == E:
-                cast_w(E, 1, on_scalar, 2, 3)
-                cast_w(E, 1, on_vector, 0, 2)
-                quantize_w(E, 5, 6)
-                quantize_w(E, 3, 5)
+                cast_w(E, 1)
+                quantize_w(E, 2, 6)
             else:
                 cast_w(e + 1, 1)
                 quantize_w(e + 1, 0, 2)
@@ -213,20 +218,11 @@ def tile_moe_shr_lin_bias_kernel(tc, xT, w, b, gate, offs, out):
                 accs = multiply_slots(e + 1)
 
         result = keep.tile([P, NT, T], F32, name="result")
-        ys = keep.tile([P, BANK], F32, name="ys")
-        last = NT - 1
-        pieces = [(last, 0, BANK)] + [(m, lo, hi) for m in range(last) for lo, hi in ((0, BANK), (BANK, T))]
-        for m, lo, hi in pieces + [(last, BANK, T)]:
-            shared = psum.tile([P, hi - lo], F32, name=f"shared{m}_{lo}")
-            product(shared[:], E, m, x_codes, x_scales, lo, hi)
-            if (m, lo) == (last, 0):
-                nc.scalar.activation(ys[:], shared[:], IDENT, bias=bias[:, m, E:E + 1])
-                nc.gpsimd.tensor_tensor(result[:, m, lo:hi], ys[:], routed[m][:, lo:hi], ADD)
-            else:
+        for m in range(NT):
+            for lo, hi in ((0, BANK), (BANK, T)):
+                shared = psum.tile([P, hi - lo], F32, name=f"shared{m}_{lo}")
+                product(shared[:], E, m, x_codes, x_scales, lo, hi)
                 nc.vector.scalar_tensor_tensor(
                     result[:, m, lo:hi], shared[:], bias[:, m, E:E + 1], routed[m][:, lo:hi], ADD, ADD
                 )
-            if m < last and hi == T:
-                nc.sync.dma_start(out=out[m * P:(m + 1) * P, :], in_=result[:, m, :])
-        for lo, hi in ((0, BANK), (BANK, T)):
-            nc.sync.dma_start(out=out[last * P:, lo:hi], in_=result[:, last, lo:hi])
+                nc.sync.dma_start(out=out[m * P:(m + 1) * P, lo:hi], in_=result[:, m, lo:hi])

@@ -176,7 +176,7 @@ def tile_moe_shr_lin_bias_kernel(tc, xT, w, b, gate, offs, out):
             return accs
 
         def y_of(e, m):
-            return w_raw[e + 1][min(m, 1)][:, PACK - 1, m * P:(m + 1) * P]
+            return w_raw[e + 1][min(m, 1)][:, m, :C]
 
         def add_bias(e, accs, m):
             nc.scalar.activation(y_of(e, m), accs[m], IDENT, bias=bias[:, m, e:e + 1])
@@ -190,7 +190,8 @@ def tile_moe_shr_lin_bias_kernel(tc, xT, w, b, gate, offs, out):
             )
 
         cast_w(0, 0)
-        cast_w(0, 1)
+        cast_w(0, 1, on_vector, 2, 3)
+        cast_w(0, 1, on_scalar, 0, 2)
         quantize_w(0, 0, 2)
         quantize_w(0, 2, 6)
         accs = multiply_slots(0)
@@ -199,18 +200,18 @@ def tile_moe_shr_lin_bias_kernel(tc, xT, w, b, gate, offs, out):
         quantize_tokens(1, 0, 512)
         quantize_tokens(1, 512, T)
         for e in range(E):
+            split = NT if e == 0 else NT - 1
             cast_w(e + 1, 0)
             add_bias(e, accs, 0)
             if e + 1 == E:
                 quantize_w(E, 0, 2)
+            if split < NT:
+                cast_w(e + 1, 1, on_vector, split, NT)
             scatter(e, 0)
-            if e + 1 == E:
-                cast_w(E, 1)
-                quantize_w(E, 2, 6)
-            else:
-                cast_w(e + 1, 1)
+            cast_w(e + 1, 1, on_scalar, 0, split)
+            if e + 1 < E:
                 quantize_w(e + 1, 0, 2)
-                quantize_w(e + 1, 2, 6)
+            quantize_w(e + 1, 2, 6)
             for m in range(1, NT):
                 add_bias(e, accs, m)
                 scatter(e, m)

from contextlib import ExitStack

import concourse.mybir as mybir

K, T, E, C, N = 1024, 768, 4, 128, 384
S = E * C

F32 = mybir.dt.float32
BF16 = mybir.dt.bfloat16
U32 = mybir.dt.uint32
U16 = mybir.dt.uint16
U8 = mybir.dt.uint8
FP8X4 = mybir.dt.float8_e4m3fn_x4
ADD = mybir.AluOpType.add
MULT = mybir.AluOpType.mult
IDENT = mybir.ActivationFunctionType.Identity

P = 128
PACK = 4
K_PASS = P * PACK
PASSES = K // K_PASS
NT = N // P
BANK = 512

FLOPS = 2 * K * N * (S + T)


def tile_moe_shr_lin_bias_kernel(tc, xT, w, b, gate, offs, out):
    nc = tc.nc
    with ExitStack() as ctx:
        keep = ctx.enter_context(tc.tile_pool(name="keep", bufs=1))
        psum = ctx.enter_context(tc.psum_pool(name="psum", bufs=1))

        offsets = keep.tile([P, S // 16], U16, name="offsets")
        x_raw = [[keep.tile([P, 2, T], F32, name=f"x_raw{g}{u}") for u in range(2)] for g in range(PASSES)]
        w_raw = [[keep.tile([P, PACK, N], F32, name=f"w_raw{e}{g}") for g in range(PASSES)] for e in range(E + 1)]
        bias = keep.tile([P, NT, 8], F32, name="bias")
        gates = keep.tile([P, NT, S], F32, name="gates")

        def load_x(g, u, lo=0, hi=T):
            rows = xT[g * K_PASS:(g + 1) * K_PASS, :].rearrange("(p j) t -> p j t", j=PACK)
            nc.sync.dma_start(out=x_raw[g][u][:, :, lo:hi], in_=rows[:, 2 * u:2 * u + 2, lo:hi])

        def load_w(e, g):
            rows = w[e, g * K_PASS:(g + 1) * K_PASS, :].rearrange("(p j) n -> p j n", j=PACK)
            nc.sync.dma_start(out=w_raw[e][g][:], in_=rows)

        load_x(0, 0, 0, T // 2)
        load_x(0, 0, T // 2, T)
        nc.sync.dma_start(offsets[:], offs)
        load_x(0, 1)
        load_x(1, 0)
        load_x(1, 1)
        load_w(0, 0)
        load_w(0, 1)
        gate_rows = gate.rearrange("(m p) s -> p m s", p=P)
        half = S // 2
        load_w(1, 0)
        nc.sync.dma_start(out=bias[:, :, :E + 1], in_=b.rearrange("(m p) e -> p m e", p=P))
        nc.sync.dma_start(out=gates[:, :1, :half], in_=gate_rows[:, :1, :half])
        load_w(1, 1)
        nc.sync.dma_start(out=gates[:, 1:, :half], in_=gate_rows[:, 1:, :half])
        load_w(2, 0)
        load_w(2, 1)
        nc.sync.dma_start(out=gates[:, :1, half:], in_=gate_rows[:, :1, half:])
        load_w(3, 0)
        load_w(3, 1)
        nc.sync.dma_start(out=gates[:, 1:, half:], in_=gate_rows[:, 1:, half:])
        load_w(4, 0)
        load_w(4, 1)

        warm = keep.tile([P, 8], F32, name="warm")
        warm_out = keep.tile([P, 8], F32, name="warm_out")
        nc.vector.memset(warm[:], 0.0)
        nc.scalar.activation(warm_out[:], warm[:], IDENT, bias=warm[:, 0:1])
        routed = [keep.tile([P, T], F32, name=f"routed{m}") for m in range(NT)]
        for m in range(NT):
            nc.vector.memset(routed[m][:], 0.0)

        x_pairs = [keep.tile([P, 2, T, 2], BF16, name=f"x_pairs{g}") for g in range(PASSES)]
        s_pairs = [keep.tile([P, 2, S, 2], BF16, name=f"s_pairs{g}") for g in range(PASSES)]
        w_quad = [keep.tile([P, NT * PASSES, P, PACK], BF16, name=f"w_quad{e}", align_bytes=64) for e in range(E + 1)]
        x_quad0 = keep.tile([P, T, 2, 2], BF16, name="x_quad0", align_bytes=64)
        w0_bytes = w_quad[0][:].rearrange("p q n j -> p (q n j)")
        x_quad = [x_quad0[:], w0_bytes.rearrange("p (c u e) -> p c u e", u=2, e=2)]
        s_quad = [keep.tile([P, S, 2, 2], BF16, name=f"s_quad{g}", align_bytes=64) for g in range(PASSES)]
        x_codes = keep.tile([P, PASSES, T], U32, name="x_codes", align_bytes=64)
        x_scales = keep.tile([P, PASSES, T], U8, name="x_scales", align_bytes=64)
        s_codes = keep.tile([P, PASSES, S], U32, name="s_codes", align_bytes=64)
        s_scales = keep.tile([P, PASSES, S], U8, name="s_scales", align_bytes=64)

        def cast_x(copy, g, u, lo, hi):
            copy(out=x_pairs[g][:, u, lo:hi, :], in_=x_raw[g][u][:, :, lo:hi].rearrange("p e t -> p t e"))

        def gather(g, u):
            window = x_pairs[g][:, u, :, :].rearrange("p t e -> p (t e)").bitcast(U32)
            dst = s_pairs[g][:, u, :, :].rearrange("p s e -> p (s e)").bitcast(U32)
            nc.vector.tensor_copy(dst, window.indirect(offsets[:]))

        def quantize(codes, scales, quad, lo, hi):
            nc.vector.quantize_mx(
                out=codes[:, lo:hi].bitcast(FP8X4), scales=scales[:, lo:hi], in_=quad[:, PACK * lo:PACK * hi]
            )

        def join_pairs(copy, quad, pairs, lo, hi):
            copy(out=quad[:, lo:hi, :, :], in_=pairs[:, :, lo:hi, :].rearrange("p u c e -> p c u e"))

        def flat(quad):
            return quad.rearrange("p c u e -> p (c u e)")

        def quantize_tokens(g, lo, hi):
            quantize(x_codes[:, g, :], x_scales[:, g, :], flat(x_quad[g]), lo, hi)

        def quantize_slots(g):
            quantize(s_codes[:, g, :], s_scales[:, g, :], flat(s_quad[g][:]), 0, S)

        on_vector, on_scalar = nc.vector.tensor_copy, nc.scalar.copy
        cast_x(on_vector, 0, 0, 0, 384)
        cast_x(on_vector, 0, 0, 384, 640)
        cast_x(on_scalar, 0, 0, 640, T)
        gather(0, 0)
        cast_x(on_vector, 0, 1, 0, 512)
        cast_x(on_scalar, 0, 1, 512, T)
        gather(0, 1)
        join_pairs(on_vector, x_quad[0], x_pairs[0], 0, 512)
        join_pairs(on_scalar, x_quad[0], x_pairs[0], 512, T)
        join_pairs(on_vector, s_quad[0], s_pairs[0], 0, S)
        for u in range(2):
            cast_x(on_scalar, 1, u, 0, T)
            gather(1, u)
        quantize_tokens(0, 0, 512)
        quantize_slots(0)
        join_pairs(on_vector, s_quad[1], s_pairs[1], 0, S)
        quantize_tokens(0, 512, T)
        quantize_slots(1)

        w_codes = [keep.tile([P, PASSES * N], U32, name=f"w_codes{e}", align_bytes=64) for e in range(E + 1)]
        w_scales = [keep.tile([P, PASSES * N], U8, name=f"w_scales{e}", align_bytes=64) for e in range(E + 1)]

        def block(e, m, g):
            return g * NT + m if e == E else m * PASSES + g

        def cast_w(e, g, copy=on_scalar, lo=0, hi=NT):
            if e == E:
                dst = w_quad[e][:, g * NT:(g + 1) * NT, :, :]
            else:
                dst = w_quad[e][:, g::PASSES, :, :]
            copy(
                out=dst[:, lo:hi, :, :].rearrange("p m (c i) j -> p m c j i", i=4),
                in_=w_raw[e][g][:, :, lo * P:hi * P].rearrange("p j (m c i) -> p m c j i", c=P // 4, i=4),
            )

        def quantize_w(e, lo, hi):
            quad = w_quad[e][:].rearrange("p q n j -> p (q n j)")
            quantize(w_codes[e], w_scales[e], quad, lo * P, hi * P)

        def product(acc, e, m, codes, scales, lo, hi):
            for g in range(PASSES):
                cols = slice(block(e, m, g) * P, (block(e, m, g) + 1) * P)
                nc.tensor.matmul_mx(
                    out=acc,
                    lhsT=w_codes[e][:, cols].bitcast(FP8X4),
                    lhsT_scale=w_scales[e][:, cols],
                    rhs=codes[:, g, lo:hi].bitcast(FP8X4),
                    rhs_scale=scales[:, g, lo:hi],
                    start=(g == 0),
                    stop=(g == PASSES - 1),
                )

        def multiply_slots(e):
            first = psum.tile([P, C], F32, name="first")
            rest = psum.tile([P, NT - 1, C], F32, name="rest")
            accs = [first[:]] + [rest[:, m, :] for m in range(NT - 1)]
            for m in range(NT):
                product(accs[m], e, m, s_codes, s_scales, e * C, (e + 1) * C)
            return accs

        def y_of(e, m):
            return w_raw[e + 1][min(m, 1)][:, m, :C]

        def add_bias(e, accs, m):
            nc.scalar.activation(y_of(e, m), accs[m], IDENT, bias=bias[:, m, e:e + 1])

        def scatter(e, m):
            nc.vector.tensor_tensor(
                routed[m][:].indirect(offsets[:, e * C // 16:(e + 1) * C // 16]),
                y_of(e, m),
                gates[:, m, e * C:(e + 1) * C],
                MULT,
            )

        cast_w(0, 0)
        cast_w(0, 1, on_vector, 2, 3)
        cast_w(0, 1, on_scalar, 0, 2)
        quantize_w(0, 0, 2)
        quantize_w(0, 2, 6)
        accs = multiply_slots(0)
        join_pairs(on_vector, x_quad[1], x_pairs[1], 0, 512)
        join_pairs(on_vector, x_quad[1], x_pairs[1], 512, T)
        quantize_tokens(1, 0, 512)
        quantize_tokens(1, 512, T)
        for e in range(E):
            split = NT if e == 0 else NT - 1
            cast_w(e + 1, 0)
            add_bias(e, accs, 0)
            if e + 1 == E:
                quantize_w(E, 0, 2)
            if split < NT:
                cast_w(e + 1, 1, on_vector, split, NT)
            scatter(e, 0)
            cast_w(e + 1, 1, on_scalar, 0, split)
            if e + 1 < E:
                quantize_w(e + 1, 0, 2)
            quantize_w(e + 1, 2, 6)
            for m in range(1, NT):
                add_bias(e, accs, m)
                scatter(e, m)
            if e + 1 < E:
                accs = multiply_slots(e + 1)

        result = keep.tile([P, NT, T], F32, name="result")
        for m in range(NT):
            for lo, hi in ((0, BANK), (BANK, T)):
                shared = psum.tile([P, hi - lo], F32, name=f"shared{m}_{lo}")
                product(shared[:], E, m, x_codes, x_scales, lo, hi)
                nc.vector.scalar_tensor_tensor(
                    result[:, m, lo:hi], shared[:], bias[:, m, E:E + 1], routed[m][:, lo:hi], ADD, ADD
                )
                nc.sync.dma_start(out=out[m * P:(m + 1) * P, lo:hi], in_=result[:, m, lo:hi])
